import numpy as np
import ml_dtypes


def mxq(x, axis, fmt="e4m3"):
    dtype, down = {"e4m3": (ml_dtypes.float8_e4m3fn, 7), "e5m2": (ml_dtypes.float8_e5m2, 14)}[fmt]
    v = np.moveaxis(np.asarray(x, np.float32).astype(ml_dtypes.bfloat16).astype(np.float64), axis, -1)
    blocks = v.reshape(v.shape[:-1] + (-1, 32))
    amax = np.abs(blocks).max(-1, keepdims=True)
    byte = np.maximum(np.where(amax > 0, np.frexp(amax)[1] - 1 + 127, 0) - down, 1)
    scale = np.exp2(byte - 127.0)
    codes = (blocks / scale).astype(np.float32).astype(dtype).astype(np.float64)
    return np.moveaxis((codes * scale).reshape(v.shape), -1, axis)


WIDE = False


def mx_kscale(k):
    if not WIDE:
        return np.ones(k)
    levels = np.array([10, -10, 5, -5, 0])
    if k % 512:
        return np.exp2(np.random.permutation(np.resize(levels, k // 32))).repeat(32)
    a = np.empty((k // 512, 16))
    for p in range(k // 512):
        a[p, :8] = np.random.permutation(np.resize(levels, 8))
        for g in range(8):
            far = levels[np.abs(levels - a[p, g]) >= 10]
            a[p, g + 8] = far[np.random.randint(len(far))]
    return np.exp2(a.ravel()).repeat(32)


def f64(x):
    return np.asarray(x).astype(np.float64)


def striped(idx):
    return np.tile(np.asarray(idx).reshape(-1, 16).T, (8, 1)).astype(np.uint16)


def unstriped(offs):
    return offs[:16].T.reshape(-1).astype(np.int64)


E2M1 = np.array([0.0, 0.5, 1.0, 1.5, 2.0, 3.0, 4.0, 6.0, -0.0, -0.5, -1.0, -1.5, -2.0, -3.0, -4.0, -6.0])


def pack_weight(w, fmt):
    k, n = w.shape
    w = f64(np.asarray(w, np.float32).astype(ml_dtypes.bfloat16)).reshape(k // 32, 32, n)
    amax = np.abs(w).max(1)
    if fmt == "e4m3":
        byte = np.frexp(amax)[1] - 1 + 127 - 7
    else:
        mant, ex = np.frexp(amax / 6.0)
        byte = np.where(mant > 0.5, ex, ex - 1) + 127
    byte = np.clip(np.where(amax > 0, byte, 1), 1, 254)
    scaled = (w * np.exp2(127.0 - byte)[:, None, :]).reshape(k, n).astype(np.float32)
    by_word = np.ascontiguousarray(scaled.reshape(k // 512, 128, 4, n).transpose(0, 1, 3, 2))
    if fmt == "e4m3":
        words = by_word.astype(ml_dtypes.float8_e4m3fn).view(np.uint8)
    else:
        c = by_word.astype(ml_dtypes.float4_e2m1fn).view(np.uint8) & 0xF
        words = (c[..., 0::2] | (c[..., 1::2] << 4)).reshape(k // 512, 128, 2 * n)
    return np.ascontiguousarray(words), np.ascontiguousarray(byte.astype(np.uint8).reshape(k // 512, 16, n))


def unpack_weight(words, scales, fmt):
    g, _, n = scales.shape
    words = np.ascontiguousarray(words).reshape(g, 128, n, -1)
    if fmt == "e4m3":
        vals = words.view(ml_dtypes.float8_e4m3fn).astype(np.float64)
    else:
        nib = np.empty((g, 128, n, 4), np.uint8)
        nib[..., 0::2] = words & 0xF
        nib[..., 1::2] = words >> 4
        vals = E2M1[nib]
    vals = vals * np.repeat(np.exp2(scales.astype(np.float64) - 127.0), 8, axis=1)[..., None]
    return vals.transpose(0, 1, 3, 2).reshape(g * 512, n)


D, T, I, Q, E, G = 512, 2048, 512, 256, 512, 8


def setup_inputs():
    n = np.random.standard_normal
    idx = np.random.permutation(T)[:I]
    fd = mx_kscale(D)
    fi = mx_kscale(I)
    ti = np.ones(T)
    ti[idx] = fi
    keysp = pack_weight(n((D, T)) / fd[:, None], "e2m1")
    return {
        "query": (n((D, Q)) * 0.5 / np.sqrt(D) * fd[:, None]).astype(np.float32),
        "keys_words": keysp[0],
        "keys_scales": keysp[1],
        "size": (np.random.uniform(0.5, 2.0, (1, I)) * fi).astype(np.float32),
        "vals": (n((E, T)) / ti).astype(np.float32),
        "target": (n((Q, E)) * 0.06).astype(np.float32),
        "fw": (np.random.uniform(0.3, 1.5, (1, E))).astype(np.float32),
        "tol": (0.2 * n((Q, G))).astype(np.float32),
        "offs": striped(idx),
    }


def reference(query, keys_words, keys_scales, size, vals, target, fw, tol, offs):
    idx = unstriped(offs)
    keysu = unpack_weight(keys_words, keys_scales, "e2m1")
    queryq = mxq(f64(query), 0, "e4m3")
    keysidxg = keysu[:, idx]
    a = queryq.T @ keysidxg
    p = np.exp(a - np.max(a, axis=1, keepdims=True))
    w = p * f64(size) / np.sum(p, axis=1, keepdims=True)
    wt = w.T
    vt = f64(vals)[:, idx].T
    wtq = mxq(wt, 0, "e4m3")
    vtq = mxq(vt, 0, "e4m3")
    o = wtq.T @ vtq
    y = np.sqrt((np.square(o - f64(target)) * f64(fw)).reshape(Q, G, E // G).mean(axis=2)) * 16.0 - f64(tol)
    return y

@@ -1,0 +1,240 @@
+from contextlib import ExitStack
+
+import concourse.mybir as mybir
+
+D, T, I, Q, E, G = 512, 2048, 512, 256, 512, 8
+FLOPS = 2 * Q * I * D + 2 * Q * I * E
+
+F32 = mybir.dt.float32
+BF16 = mybir.dt.bfloat16
+I32 = mybir.dt.int32
+U32 = mybir.dt.uint32
+U16 = mybir.dt.uint16
+U8 = mybir.dt.uint8
+FP8X4 = mybir.dt.float8_e4m3fn_x4
+FP4X4 = mybir.dt.float4_e2m1fn_x4
+ALU = mybir.AluOpType
+ACT = mybir.ActivationFunctionType
+AXIS = mybir.AxisListType
+
+P = 128
+PACK = 4
+HALVES = Q // P
+BLOCKS = E // P
+
+
+def tile_attend_readerrors_kernel(tc, query, keys_words, keys_scales, size, vals, target, fw, tol, offs, out):
+    nc = tc.nc
+    with ExitStack() as ctx:
+        keep = ctx.enter_context(tc.tile_pool(name="keep", bufs=1))
+        psum = ctx.enter_context(tc.psum_pool(name="psum", bufs=1))
+
+        offsets = keep.tile([P, I // 16], U16, name="offsets")
+        nc.sync.dma_start(offsets[:], offs)
+
+        key_bytes = keep.tile([P, T], U8, name="key_bytes", tag="key_bytes")
+        nc.gpsimd.memset(key_bytes[:].bitcast(I32), 0)
+        for quad in range(4):
+            nc.scalar.dma_start(
+                key_bytes[32 * quad : 32 * quad + 4, :].bitcast(I32),
+                keys_scales[0, 4 * quad : 4 * quad + 4, :].bitcast(I32),
+            )
+        key_words = keep.tile([P, T], U16, name="key_words", tag="key_words", align_bytes=64)
+        nc.sync.dma_start(key_words[:].bitcast(I32), keys_words[0].bitcast(I32))
+        q_raw = keep.tile([P, PACK, Q], F32, name="q_raw", tag="q_raw")
+        nc.sync.dma_start(q_raw[:], query.rearrange("(p t) q -> p t q", t=PACK))
+
+        size_col = keep.tile([P, PACK], F32, name="size_col")
+        nc.sync.dma_start(size_col[:], size.rearrange("o (p t) -> (o p) t", t=PACK))
+        zeros = keep.tile([P, P], F32, name="zeros", tag="zeros", align_bytes=64)
+        nc.gpsimd.memset(zeros[:], 0.0)
+        ident = keep.tile([P, P], F32, name="ident")
+        nc.gpsimd.affine_select(
+            out=ident[:], in_=zeros[:], compare_op=ALU.not_equal, fill=1.0, base=0, pattern=[[-1, P]], channel_multiplier=1
+        )
+
+        vals_by_block = vals.rearrange("(p j) t -> j p t", j=BLOCKS)
+        v_pool = [keep.tile([P, T], F32, name="v_pool0", tag="zeros", align_bytes=64)]
+        nc.sync.dma_start(v_pool[0][:], vals_by_block[0])
+        kg_words = keep.tile([P, I], U16, name="kg_words", tag="kg_words", align_bytes=64)
+        nc.vector.tensor_copy(kg_words[:], key_words[:].indirect(offsets[:]))
+        kg_bytes = keep.tile([P, I], U8, name="kg_bytes", align_bytes=64)
+        nc.vector.tensor_copy(kg_bytes[:], key_bytes[:].indirect(offsets[:]))
+
+        v_pool.append(keep.tile([P, T], F32, name="v_pool1", tag="key_words", align_bytes=64))
+        nc.sync.dma_start(v_pool[1][:], vals_by_block[1])
+        fw_col = keep.tile([P, BLOCKS], F32, name="fw_col", tag="key_bytes")
+        nc.sync.dma_start(fw_col[:], fw.rearrange("o (p j) -> (o p) j", j=BLOCKS))
+
+        scores, neg_max = [], []
+        for h in range(HALVES):
+            q_bf = keep.tile([P, P * PACK], BF16, name="q_bf%d" % h, tag="q_bf%d" % h, align_bytes=64)
+            nc.scalar.copy(
+                q_bf[:].rearrange("p (m t) -> p m t", t=PACK),
+                q_raw[:].rearrange("p t (m h) -> p h m t", h=HALVES)[:, h],
+            )
+            q_codes = keep.tile([P, P], U32, name="q_codes%d" % h, tag="q_codes%d" % h, align_bytes=64)
+            q_bytes = keep.tile([P, P], U8, name="q_bytes%d" % h, align_bytes=64)
+            nc.vector.quantize_mx(out=q_codes[:].bitcast(FP8X4), scales=q_bytes[:], in_=q_bf[:])
+            bank = psum.tile([P, I], F32, name="scores%d" % h, tag="row%d" % h)
+            nc.tensor.matmul_mx(
+                out=bank[:],
+                lhsT=q_codes[:].bitcast(FP8X4),
+                lhsT_scale=q_bytes[:],
+                rhs=kg_words[:].bitcast(FP4X4),
+                rhs_scale=kg_bytes[:],
+                start=True,
+                stop=True,
+            )
+            scores.append(bank)
+        tgt = keep.tile([P, HALVES, E], F32, name="tgt", tag="q_raw")
+        nc.sync.dma_start(tgt[:], target.rearrange("(m h) e -> m h e", h=HALVES))
+        tol_sb = keep.tile([P, HALVES * G], F32, name="tol_sb", tag="q_bf0", align_bytes=64)
+        nc.sync.dma_start(tol_sb[:], tol.rearrange("(m h) g -> m (h g)", h=HALVES))
+        v_pool.append(keep.tile([P, T], F32, name="v_pool2", tag="q_bf1", align_bytes=64))
+        nc.sync.dma_start(v_pool[2][:], vals_by_block[2])
+        v_pool.append(keep.tile([P, T], F32, name="v_pool3", tag="kg_words", align_bytes=64))
+        nc.sync.dma_start(v_pool[3][:], vals_by_block[3])
+        for h in range(HALVES):
+            nm = keep.tile([P, 1], F32, name="neg_max%d" % h)
+            nc.vector.tensor_reduce(nm[:], scores[h][:], AXIS.X, ALU.max, negate=True)
+            neg_max.append(nm)
+
+        size_row = psum.tile([P, PACK, P], F32, name="size_row", tag="spread")
+        for t in range(PACK):
+            nc.tensor.transpose(size_row[:, t, :], size_col[:, t : t + 1].to_broadcast([P, P]), ident[:])
+
+        picks = []
+        pick_tags = ["q_codes1", "probs1", "v_turned1", "tgt_turned0"]
+
+        def gather_values(j):
+            picked = keep.tile([P, I], BF16, name="v_picked%d" % j, tag=pick_tags[j], align_bytes=64)
+            nc.vector.tensor_copy(picked[:], v_pool[j][:].indirect(offsets[:]))
+            picks.append(picked)
+            return picked
+
+        def turn(rows_bf, name, tag):
+            words = rows_bf[:].bitcast(F32)
+            bank = psum.tile([P, 2, P], F32, name=name + "_bank", tag=tag)
+            for u in range(2):
+                nc.tensor.transpose(bank[:, u, :], words[:, u::2], ident[:])
+            grouped = keep.tile([P, P * PACK], BF16, name=name, tag=name, align_bytes=64)
+            nc.scalar.copy(
+                grouped[:].bitcast(F32).rearrange("p (r u) -> p r u", u=2),
+                bank[:].rearrange("p u r -> p r u"),
+            )
+            return grouped
+
+        probs, sums = [], []
+        for h in range(HALVES):
+            p_h = keep.tile([P, I], F32, name="probs%d" % h, tag="probs%d" % h, align_bytes=64)
+            s_h = keep.tile([P, 1], F32, name="sums%d" % h)
+            nc.scalar.activation(p_h[:], scores[h][:], ACT.Exp, bias=neg_max[h][:], accum_out=s_h[:])
+            probs.append(p_h)
+            sums.append(s_h)
+
+        v_turned = [turn(gather_values(0), "v_turned0", "turn_v")]
+
+        w_turned = []
+        for h in range(HALVES):
+            inv = keep.tile([P, 1], F32, name="inv%d" % h)
+            nc.vector.reciprocal(inv[:], sums[h][:])
+            w_bf = keep.tile([P, I], BF16, name="w_bf%d" % h)
+            nc.vector.scalar_tensor_tensor(
+                w_bf[:].rearrange("q (p t) -> q p t", t=PACK),
+                probs[h][:].rearrange("q (p t) -> q p t", t=PACK),
+                inv[:],
+                size_row[:].rearrange("q t p -> q p t"),
+                ALU.mult,
+                ALU.mult,
+            )
+            w_turned.append(turn(w_bf, "w_turned%d" % h, "turn_w%d" % h))
+        v_turned.append(turn(gather_values(1), "v_turned1", "turn_v"))
+        w_codes = keep.tile([P, Q], U32, name="w_codes", tag="key_words", align_bytes=64)
+        w_bytes = keep.tile([P, Q], U8, name="w_bytes", align_bytes=64)
+        for h in range(HALVES):
+            nc.vector.quantize_mx(
+                out=w_codes[:, h * P : (h + 1) * P].bitcast(FP8X4),
+                scales=w_bytes[:, h * P : (h + 1) * P],
+                in_=w_turned[h][:],
+            )
+
+        tgt_turned = []
+        for pair in range(BLOCKS // 2):
+            bank = psum.tile([P, 2, HALVES, P], F32, name="tgt_bank%d" % pair, tag="turn_w%d" % pair)
+            for jj in range(2):
+                for h in range(HALVES):
+                    nc.tensor.transpose(bank[:, jj, h, :], tgt[:, h, 2 * pair + jj :: BLOCKS], ident[:])
+            turned = keep.tile([P, 2, Q], F32, name="tgt_turned%d" % pair, tag="tgt_turned%d" % pair, align_bytes=64)
+            nc.scalar.copy(turned[:], bank[:].rearrange("p j h m -> p j (h m)"))
+            tgt_turned.append(turned)
+
+        totals = [psum.tile([P, P], F32, name="totals%d" % h, tag="row%d" % h) for h in range(HALVES)]
+        read_tags = ["read0", "read1", "turn_w0", "spread"]
+
+        def read_out(j):
+            if j == 2:
+                v_codes = keep.tile([P, P], U32, name="v_codes%d" % j, tag="kg_words", align_bytes=64)
+            else:
+                v_codes = keep.tile([P, P], U32, name="v_codes%d" % j, align_bytes=64)
+            v_bytes = keep.tile([P, P], U8, name="v_bytes%d" % j, align_bytes=64)
+            nc.vector.quantize_mx(out=v_codes[:].bitcast(FP8X4), scales=v_bytes[:], in_=v_turned[j][:])
+            reads = psum.tile([P, Q], F32, name="reads%d" % j, tag=read_tags[j])
+            nc.tensor.matmul_mx(
+                out=reads[:],
+                lhsT=v_codes[:].bitcast(FP8X4),
+                lhsT_scale=v_bytes[:],
+                rhs=w_codes[:].bitcast(FP8X4),
+                rhs_scale=w_bytes[:],
+                start=True,
+                stop=True,
+            )
+            return reads
+
+        def add_squares(j, reads):
+            diffs = []
+            for h in range(HALVES):
+                diff = keep.tile([P, P], F32, name="diff%d_%d" % (j, h))
+                nc.vector.tensor_tensor(
+                    diff[:], reads[:, h * P : (h + 1) * P], tgt_turned[j // 2][:, j % 2, h * P : (h + 1) * P], ALU.subtract
+                )
+                diffs.append(diff)
+            for h in range(HALVES):
+                sq = keep.tile([P, P], F32, name="sq%d_%d" % (j, h))
+                nc.vector.scalar_tensor_tensor(sq[:], diffs[h][:], fw_col[:, j : j + 1], diffs[h][:], ALU.mult, ALU.mult)
+                nc.tensor.matmul(totals[h][:], sq[:], ident[:], start=(j == 0), stop=(j == BLOCKS - 1), is_transpose=True)
+
+        def add_squares_early(j, reads):
+            if j == 0:
+                diff = keep.tile([P, Q], F32, name="diff%d" % j, tag="q_bf1", align_bytes=64)
+            else:
+                diff = keep.tile([P, Q], F32, name="diff%d" % j)
+            nc.vector.tensor_tensor(diff[:], reads[:], tgt_turned[j // 2][:, j % 2, :], ALU.subtract)
+            plain = keep.tile([P, Q], F32, name="plain%d" % j)
+            nc.scalar.activation(plain[:], diff[:], ACT.Square)
+            sq = keep.tile([P, Q], F32, name="sq%d" % j)
+            nc.scalar.activation(sq[:], plain[:], ACT.Copy, scale=fw_col[:, j : j + 1])
+            for h in range(HALVES):
+                nc.tensor.matmul(
+                    totals[h][:], sq[:, h * P : (h + 1) * P], ident[:], start=(j == 0), stop=False, is_transpose=True
+                )
+
+        reads0 = read_out(0)
+        reads1 = read_out(1)
+        v_turned.append(turn(gather_values(2), "v_turned2", "turn_v"))
+        add_squares_early(0, reads0)
+        add_squares_early(1, reads1)
+        v_turned.append(turn(gather_values(3), "v_turned3", "turn_v"))
+        add_squares_early(2, read_out(2))
+        add_squares(3, read_out(3))
+
+        block_sums = keep.tile([P, HALVES, G], F32, name="block_sums")
+        for h in range(HALVES):
+            nc.vector.tensor_reduce(
+                block_sums[:, h, :], totals[h][:].rearrange("m (g r) -> m g r", g=G), AXIS.X, ALU.add
+            )
+        roots = keep.tile([P, HALVES * G], F32, name="roots")
+        nc.scalar.activation(roots[:], block_sums[:].rearrange("m h g -> m (h g)"), ACT.Sqrt, scale=16.0 * 16.0 / (E // G))
+        result = keep.tile([P, HALVES * G], F32, name="result")
+        nc.vector.tensor_tensor(result[:], roots[:], tol_sb[:], ALU.subtract)
+        nc.sync.dma_start(out.rearrange("(m h) g -> m (h g)", h=HALVES), result[:])

@@ -1,6 +1,7 @@
 from contextlib import ExitStack
 
 import concourse.mybir as mybir
+from concourse.masks import make_identity
 
 D, T, I, Q, E, G = 512, 2048, 512, 256, 512, 8
 FLOPS = 2 * Q * I * D + 2 * Q * I * E
@@ -27,6 +28,7 @@ def tile_attend_readerrors_kernel(tc, query, keys_words, keys_scales, size, vals
     nc = tc.nc
     with ExitStack() as ctx:
         keep = ctx.enter_context(tc.tile_pool(name="keep", bufs=1))
+        staged = ctx.enter_context(tc.tile_pool(name="staged", bufs=1))
         psum = ctx.enter_context(tc.psum_pool(name="psum", bufs=1))
 
         offsets = keep.tile([P, I // 16], U16, name="offsets")
@@ -46,25 +48,26 @@ def tile_attend_readerrors_kernel(tc, query, keys_words, keys_scales, size, vals
 
         size_col = keep.tile([P, PACK], F32, name="size_col")
         nc.sync.dma_start(size_col[:], size.rearrange("o (p t) -> (o p) t", t=PACK))
-        zeros = keep.tile([P, P], F32, name="zeros", tag="zeros", align_bytes=64)
-        nc.gpsimd.memset(zeros[:], 0.0)
         ident = keep.tile([P, P], F32, name="ident")
-        nc.gpsimd.affine_select(
-            out=ident[:], in_=zeros[:], compare_op=ALU.not_equal, fill=1.0, base=0, pattern=[[-1, P]], channel_multiplier=1
-        )
+        make_identity(nc, ident[:])
 
         vals_by_block = vals.rearrange("(p j) t -> j p t", j=BLOCKS)
-        v_pool = [keep.tile([P, T], F32, name="v_pool0", tag="zeros", align_bytes=64)]
+        v_pool = [staged.tile([P, T], F32, name="v_pool%d" % j, offset=8192 * j) for j in range(BLOCKS)]
+        tgt = keep.tile([P, HALVES, E], F32, name="tgt")
+        fw_col = keep.tile([P, BLOCKS], F32, name="fw_col")
+        tol_sb = keep.tile([P, HALVES * G], F32, name="tol_sb")
         nc.sync.dma_start(v_pool[0][:], vals_by_block[0])
-        kg_words = keep.tile([P, I], U16, name="kg_words", tag="kg_words", align_bytes=64)
+        nc.sync.dma_start(v_pool[1][:], vals_by_block[1])
+        nc.sync.dma_start(tgt[:], target.rearrange("(m h) e -> m h e", h=HALVES))
+        nc.sync.dma_start(fw_col[:], fw.rearrange("o (p j) -> (o p) j", j=BLOCKS))
+        nc.sync.dma_start(tol_sb[:], tol.rearrange("(m h) g -> m (h g)", h=HALVES))
+        nc.sync.dma_start(v_pool[2][:], vals_by_block[2])
+        nc.sync.dma_start(v_pool[3][:], vals_by_block[3])
+
+        kg_words = keep.tile([P, I], U16, name="kg_words", align_bytes=64)
         nc.vector.tensor_copy(kg_words[:], key_words[:].indirect(offsets[:]))
         kg_bytes = keep.tile([P, I], U8, name="kg_bytes", align_bytes=64)
         nc.vector.tensor_copy(kg_bytes[:], key_bytes[:].indirect(offsets[:]))
-
-        v_pool.append(keep.tile([P, T], F32, name="v_pool1", tag="key_words", align_bytes=64))
-        nc.sync.dma_start(v_pool[1][:], vals_by_block[1])
-        fw_col = keep.tile([P, BLOCKS], F32, name="fw_col", tag="key_bytes")
-        nc.sync.dma_start(fw_col[:], fw.rearrange("o (p j) -> (o p) j", j=BLOCKS))
 
         scores, neg_max = [], []
         for h in range(HALVES):
@@ -87,43 +90,40 @@ def tile_attend_readerrors_kernel(tc, query, keys_words, keys_scales, size, vals
                 stop=True,
             )
             scores.append(bank)
-        tgt = keep.tile([P, HALVES, E], F32, name="tgt", tag="q_raw")
-        nc.sync.dma_start(tgt[:], target.rearrange("(m h) e -> m h e", h=HALVES))
-        tol_sb = keep.tile([P, HALVES * G], F32, name="tol_sb", tag="q_bf0", align_bytes=64)
-        nc.sync.dma_start(tol_sb[:], tol.rearrange("(m h) g -> m (h g)", h=HALVES))
-        v_pool.append(keep.tile([P, T], F32, name="v_pool2", tag="q_bf1", align_bytes=64))
-        nc.sync.dma_start(v_pool[2][:], vals_by_block[2])
-        v_pool.append(keep.tile([P, T], F32, name="v_pool3", tag="kg_words", align_bytes=64))
-        nc.sync.dma_start(v_pool[3][:], vals_by_block[3])
-        for h in range(HALVES):
-            nm = keep.tile([P, 1], F32, name="neg_max%d" % h)
-            nc.vector.tensor_reduce(nm[:], scores[h][:], AXIS.X, ALU.max, negate=True)
-            neg_max.append(nm)
-
         size_row = psum.tile([P, PACK, P], F32, name="size_row", tag="spread")
         for t in range(PACK):
             nc.tensor.transpose(size_row[:, t, :], size_col[:, t : t + 1].to_broadcast([P, P]), ident[:])
 
         picks = []
-        pick_tags = ["q_codes1", "probs1", "v_turned1", "tgt_turned0"]
+        pick_tags = ["q_bf1", "q_codes1", "probs1", "q_codes0"]
 
         def gather_values(j):
-            picked = keep.tile([P, I], BF16, name="v_picked%d" % j, tag=pick_tags[j], align_bytes=64)
+            if j == 3:
+                picked = staged.tile([P, I], BF16, name="v_picked%d" % j, offset=16384)
+            else:
+                picked = keep.tile([P, I], BF16, name="v_picked%d" % j, tag=pick_tags[j], align_bytes=64)
             nc.vector.tensor_copy(picked[:], v_pool[j][:].indirect(offsets[:]))
             picks.append(picked)
             return picked
 
-        def turn(rows_bf, name, tag):
+        def turn(rows_bf, name, tag, grouped):
             words = rows_bf[:].bitcast(F32)
             bank = psum.tile([P, 2, P], F32, name=name + "_bank", tag=tag)
             for u in range(2):
                 nc.tensor.transpose(bank[:, u, :], words[:, u::2], ident[:])
-            grouped = keep.tile([P, P * PACK], BF16, name=name, tag=name, align_bytes=64)
             nc.scalar.copy(
-                grouped[:].bitcast(F32).rearrange("p (r u) -> p r u", u=2),
+                grouped.bitcast(F32).rearrange("p (r u) -> p r u", u=2),
                 bank[:].rearrange("p u r -> p r u"),
             )
-            return grouped
+
+        v_early = keep.tile([P, 2 * P * PACK], BF16, name="v_early", align_bytes=64)
+        v_late = [staged.tile([P, P * PACK], BF16, name="v_late%d" % j, offset=32768 + 1024 * j, align_bytes=64) for j in range(2)]
+        w_turned = keep.tile([P, Q * PACK], BF16, name="w_turned", align_bytes=64)
+        turn(gather_values(0), "v_turned0", "turn_v", v_early[:, 0:I])
+        for h in range(HALVES):
+            nm = keep.tile([P, 1], F32, name="neg_max%d" % h)
+            nc.vector.tensor_reduce(nm[:], scores[h][:], AXIS.X, ALU.max, negate=True)
+            neg_max.append(nm)
 
         probs, sums = [], []
         for h in range(HALVES):
@@ -132,10 +132,11 @@ def tile_attend_readerrors_kernel(tc, query, keys_words, keys_scales, size, vals
             nc.scalar.activation(p_h[:], scores[h][:], ACT.Exp, bias=neg_max[h][:], accum_out=s_h[:])
             probs.append(p_h)
             sums.append(s_h)
+        warm = keep.tile([P, 1], F32, name="warm")
+        nc.scalar.activation(warm[:], sums[HALVES - 1][:], ACT.Sqrt)
 
-        v_turned = [turn(gather_values(0), "v_turned0", "turn_v")]
 
-        w_turned = []
+        turn(gather_values(1), "v_turned1", "turn_v", v_early[:, I : 2 * I])
         for h in range(HALVES):
             inv = keep.tile([P, 1], F32, name="inv%d" % h)
             nc.vector.reciprocal(inv[:], sums[h][:])
@@ -148,20 +149,18 @@ def tile_attend_readerrors_kernel(tc, query, keys_words, keys_scales, size, vals
                 ALU.mult,
                 ALU.mult,
             )
-            w_turned.append(turn(w_bf, "w_turned%d" % h, "turn_w%d" % h))
-        v_turned.append(turn(gather_values(1), "v_turned1", "turn_v"))
-        w_codes = keep.tile([P, Q], U32, name="w_codes", tag="key_words", align_bytes=64)
+            turn(w_bf, "w_turned%d" % h, "turn_w%d" % h, w_turned[:, h * I : (h + 1) * I])
+        turn(gather_values(2), "v_turned2", "turn_v", v_late[0][:])
+        w_codes = keep.tile([P, Q], U32, name="w_codes", align_bytes=64)
         w_bytes = keep.tile([P, Q], U8, name="w_bytes", align_bytes=64)
-        for h in range(HALVES):
-            nc.vector.quantize_mx(
-                out=w_codes[:, h * P : (h + 1) * P].bitcast(FP8X4),
-                scales=w_bytes[:, h * P : (h + 1) * P],
-                in_=w_turned[h][:],
-            )
+        early_codes = keep.tile([P, 2 * P], U32, name="early_codes", align_bytes=64)
+        early_bytes = keep.tile([P, 2 * P], U8, name="early_bytes", align_bytes=64)
+        nc.vector.quantize_mx(out=early_codes[:].bitcast(FP8X4), scales=early_bytes[:], in_=v_early[:])
+        nc.vector.quantize_mx(out=w_codes[:].bitcast(FP8X4), scales=w_bytes[:], in_=w_turned[:])
 
         tgt_turned = []
         for pair in range(BLOCKS // 2):
-            bank = psum.tile([P, 2, HALVES, P], F32, name="tgt_bank%d" % pair, tag="turn_w%d" % pair)
+            bank = psum.tile([P, 2, HALVES, P], F32, name="tgt_bank%d" % pair, tag="row%d" % pair)
             for jj in range(2):
                 for h in range(HALVES):
                     nc.tensor.transpose(bank[:, jj, h, :], tgt[:, h, 2 * pair + jj :: BLOCKS], ident[:])
@@ -170,63 +169,68 @@ def tile_attend_readerrors_kernel(tc, query, keys_words, keys_scales, size, vals
             tgt_turned.append(turned)
 
         totals = [psum.tile([P, P], F32, name="totals%d" % h, tag="row%d" % h) for h in range(HALVES)]
-        read_tags = ["read0", "read1", "turn_w0", "spread"]
 
-        def read_out(j):
-            if j == 2:
-                v_codes = keep.tile([P, P], U32, name="v_codes%d" % j, tag="kg_words", align_bytes=64)
-            else:
-                v_codes = keep.tile([P, P], U32, name="v_codes%d" % j, align_bytes=64)
-            v_bytes = keep.tile([P, P], U8, name="v_bytes%d" % j, align_bytes=64)
-            nc.vector.quantize_mx(out=v_codes[:].bitcast(FP8X4), scales=v_bytes[:], in_=v_turned[j][:])
-            reads = psum.tile([P, Q], F32, name="reads%d" % j, tag=read_tags[j])
+        def read_out(reads, codes, scale_bytes):
             nc.tensor.matmul_mx(
-                out=reads[:],
-                lhsT=v_codes[:].bitcast(FP8X4),
-                lhsT_scale=v_bytes[:],
+                out=reads,
+                lhsT=codes.bitcast(FP8X4),
+                lhsT_scale=scale_bytes,
                 rhs=w_codes[:].bitcast(FP8X4),
                 rhs_scale=w_bytes[:],
                 start=True,
                 stop=True,
             )
-            return reads
 
-        def add_squares(j, reads):
-            diffs = []
-            for h in range(HALVES):
-                diff = keep.tile([P, P], F32, name="diff%d_%d" % (j, h))
-                nc.vector.tensor_tensor(
-                    diff[:], reads[:, h * P : (h + 1) * P], tgt_turned[j // 2][:, j % 2, h * P : (h + 1) * P], ALU.subtract
-                )
-                diffs.append(diff)
-            for h in range(HALVES):
-                sq = keep.tile([P, P], F32, name="sq%d_%d" % (j, h))
-                nc.vector.scalar_tensor_tensor(sq[:], diffs[h][:], fw_col[:, j : j + 1], diffs[h][:], ALU.mult, ALU.mult)
-                nc.tensor.matmul(totals[h][:], sq[:], ident[:], start=(j == 0), stop=(j == BLOCKS - 1), is_transpose=True)
+        def add_turned(j, h, squares):
+            nc.tensor.matmul(totals[h][:], squares, ident[:], start=(j == 0), stop=(j == BLOCKS - 1), is_transpose=True)
 
-        def add_squares_early(j, reads):
-            if j == 0:
-                diff = keep.tile([P, Q], F32, name="diff%d" % j, tag="q_bf1", align_bytes=64)
-            else:
-                diff = keep.tile([P, Q], F32, name="diff%d" % j)
-            nc.vector.tensor_tensor(diff[:], reads[:], tgt_turned[j // 2][:, j % 2, :], ALU.subtract)
-            plain = keep.tile([P, Q], F32, name="plain%d" % j)
-            nc.scalar.activation(plain[:], diff[:], ACT.Square)
+        def weigh_and_add(j, plain):
             sq = keep.tile([P, Q], F32, name="sq%d" % j)
-            nc.scalar.activation(sq[:], plain[:], ACT.Copy, scale=fw_col[:, j : j + 1])
+            nc.scalar.activation(sq[:], plain, ACT.Copy, scale=fw_col[:, j : j + 1])
             for h in range(HALVES):
-                nc.tensor.matmul(
-                    totals[h][:], sq[:, h * P : (h + 1) * P], ident[:], start=(j == 0), stop=False, is_transpose=True
-                )
+                add_turned(j, h, sq[:, h * P : (h + 1) * P])
 
-        reads0 = read_out(0)
-        reads1 = read_out(1)
-        v_turned.append(turn(gather_values(2), "v_turned2", "turn_v"))
-        add_squares_early(0, reads0)
-        add_squares_early(1, reads1)
-        v_turned.append(turn(gather_values(3), "v_turned3", "turn_v"))
-        add_squares_early(2, read_out(2))
-        add_squares(3, read_out(3))
+        reads_early = psum.tile([P, 2, Q], F32, name="reads_early", tag="read0")
+        for j in range(2):
+            read_out(reads_early[:, j, :], early_codes[:, j * P : (j + 1) * P], early_bytes[:, j * P : (j + 1) * P])
+
+        turn(gather_values(3), "v_turned3", "turn_v", v_late[1][:])
+
+        codes2 = staged.tile([P, P], U32, name="codes2", offset=24576, align_bytes=64)
+        bytes2 = keep.tile([P, P], U8, name="bytes2", align_bytes=64)
+        nc.vector.quantize_mx(out=codes2[:].bitcast(FP8X4), scales=bytes2[:], in_=v_late[0][:])
+        reads2 = psum.tile([P, Q], F32, name="reads2", tag="turn_w0")
+        read_out(reads2[:], codes2[:], bytes2[:])
+
+        diff_early = staged.tile([P, 2, Q], F32, name="diff_early", offset=24576 + 1024)
+        nc.vector.tensor_tensor(diff_early[:], reads_early[:], tgt_turned[0][:], ALU.subtract)
+        plain_early = staged.tile([P, 2, Q], F32, name="plain_early", offset=16384)
+        nc.scalar.activation(plain_early[:], diff_early[:], ACT.Square)
+        for j in range(2):
+            weigh_and_add(j, plain_early[:, j, :])
+
+        codes3 = keep.tile([P, P], U32, name="codes3", align_bytes=64)
+        bytes3 = keep.tile([P, P], U8, name="bytes3", align_bytes=64)
+        nc.vector.quantize_mx(out=codes3[:].bitcast(FP8X4), scales=bytes3[:], in_=v_late[1][:])
+        reads3 = psum.tile([P, Q], F32, name="reads3", tag="turn_w1")
+        read_out(reads3[:], codes3[:], bytes3[:])
+
+        diff2 = staged.tile([P, Q], F32, name="diff2", offset=32768 + 1024)
+        nc.vector.tensor_tensor(diff2[:], reads2[:], tgt_turned[1][:, 0, :], ALU.subtract)
+        plain2 = keep.tile([P, Q], F32, name="plain2")
+        nc.scalar.activation(plain2[:], diff2[:], ACT.Square)
+        weigh_and_add(2, plain2[:])
+
+        diffs = []
+        for h in range(HALVES):
+            diff = keep.tile([P, P], F32, name="diff3_%d" % h)
+            cols = slice(h * P, (h + 1) * P)
+            nc.vector.tensor_tensor(diff[:], reads3[:, cols], tgt_turned[1][:, 1, cols], ALU.subtract)
+            diffs.append(diff)
+        for h in range(HALVES):
+            sq = keep.tile([P, P], F32, name="sq3_%d" % h)
+            nc.vector.scalar_tensor_tensor(sq[:], diffs[h][:], fw_col[:, 3:4], diffs[h][:], ALU.mult, ALU.mult)
+            add_turned(3, h, sq[:])
 
         block_sums = keep.tile([P, HALVES, G], F32, name="block_sums")
         for h in range(HALVES):

@@ -21,7 +21,9 @@ AXIS = mybir.AxisListType
 P = 128
 PACK = 4
 HALVES = Q // P
+PAIRS = 2
 BLOCKS = E // P
+POOL_BYTES = 4 * T
 
 
 def tile_attend_readerrors_kernel(tc, query, keys_words, keys_scales, size, vals, target, fw, tol, offs, out):
@@ -34,81 +36,69 @@ def tile_attend_readerrors_kernel(tc, query, keys_words, keys_scales, size, vals
         offsets = keep.tile([P, I // 16], U16, name="offsets")
         nc.sync.dma_start(offsets[:], offs)
 
-        key_bytes = keep.tile([P, T], U8, name="key_bytes", tag="key_bytes")
+        key_bytes = keep.tile([P, T], U8, name="key_bytes")
         nc.gpsimd.memset(key_bytes[:].bitcast(I32), 0)
         for quad in range(4):
-            nc.scalar.dma_start(
+            (nc.scalar if quad < 2 else nc.sync).dma_start(
                 key_bytes[32 * quad : 32 * quad + 4, :].bitcast(I32),
                 keys_scales[0, 4 * quad : 4 * quad + 4, :].bitcast(I32),
             )
-        key_words = keep.tile([P, T], U16, name="key_words", tag="key_words", align_bytes=64)
+        key_words = keep.tile([P, T], U16, name="key_words")
         nc.sync.dma_start(key_words[:].bitcast(I32), keys_words[0].bitcast(I32))
-        q_raw = keep.tile([P, PACK, Q], F32, name="q_raw", tag="q_raw")
+        q_raw = keep.tile([P, PACK, Q], F32, name="q_raw")
         nc.sync.dma_start(q_raw[:], query.rearrange("(p t) q -> p t q", t=PACK))
-
         size_col = keep.tile([P, PACK], F32, name="size_col")
         nc.sync.dma_start(size_col[:], size.rearrange("o (p t) -> (o p) t", t=PACK))
+
+        vals_by_block = vals.rearrange("(b p j) t -> b j p t", b=PAIRS, j=2)
+        v_pool = [staged.tile([P, T], F32, name="v_pool%d" % n, offset=POOL_BYTES * n) for n in range(BLOCKS)]
+        tgt = keep.tile([P, HALVES, E], F32, name="tgt")
+        nc.sync.dma_start(v_pool[0][:], vals_by_block[0, 0])
+        nc.sync.dma_start(tgt[:], target.rearrange("(m h) e -> m h e", h=HALVES))
+        for n in range(1, BLOCKS):
+            nc.sync.dma_start(v_pool[n][:], vals_by_block[n // 2, n % 2])
+
         ident = keep.tile([P, P], F32, name="ident")
         make_identity(nc, ident[:])
-
-        vals_by_block = vals.rearrange("(p j) t -> j p t", j=BLOCKS)
-        v_pool = [staged.tile([P, T], F32, name="v_pool%d" % j, offset=8192 * j) for j in range(BLOCKS)]
-        tgt = keep.tile([P, HALVES, E], F32, name="tgt")
-        fw_col = keep.tile([P, BLOCKS], F32, name="fw_col")
+        fw_col = keep.tile([P, PAIRS, 2], F32, name="fw_col")
+        nc.gpsimd.dma_start(fw_col[:], fw.rearrange("o (b p j) -> (o p) b j", b=PAIRS, j=2))
         tol_sb = keep.tile([P, HALVES * G], F32, name="tol_sb")
-        nc.sync.dma_start(v_pool[0][:], vals_by_block[0])
-        nc.sync.dma_start(v_pool[1][:], vals_by_block[1])
-        nc.sync.dma_start(tgt[:], target.rearrange("(m h) e -> m h e", h=HALVES))
-        nc.sync.dma_start(fw_col[:], fw.rearrange("o (p j) -> (o p) j", j=BLOCKS))
-        nc.sync.dma_start(tol_sb[:], tol.rearrange("(m h) g -> m (h g)", h=HALVES))
-        nc.sync.dma_start(v_pool[2][:], vals_by_block[2])
-        nc.sync.dma_start(v_pool[3][:], vals_by_block[3])
+        nc.gpsimd.dma_start(tol_sb[:], tol.rearrange("(m h) g -> m (h g)", h=HALVES))
 
         kg_words = keep.tile([P, I], U16, name="kg_words", align_bytes=64)
         nc.vector.tensor_copy(kg_words[:], key_words[:].indirect(offsets[:]))
         kg_bytes = keep.tile([P, I], U8, name="kg_bytes", align_bytes=64)
         nc.vector.tensor_copy(kg_bytes[:], key_bytes[:].indirect(offsets[:]))
 
-        scores, neg_max = [], []
+        q_bf = keep.tile([P, Q * PACK], BF16, name="q_bf", tag="q_bf", align_bytes=64)
+        nc.scalar.copy(
+            q_bf[:].rearrange("p (h m t) -> p m h t", h=HALVES, t=PACK),
+            q_raw[:].rearrange("p t (m h) -> p m h t", h=HALVES),
+        )
+        q_codes = keep.tile([P, Q], U32, name="q_codes", align_bytes=64)
+        q_bytes = keep.tile([P, Q], U8, name="q_bytes", align_bytes=64)
+        nc.vector.quantize_mx(out=q_codes[:].bitcast(FP8X4), scales=q_bytes[:], in_=q_bf[:])
+        scores = []
         for h in range(HALVES):
-            q_bf = keep.tile([P, P * PACK], BF16, name="q_bf%d" % h, tag="q_bf%d" % h, align_bytes=64)
-            nc.scalar.copy(
-                q_bf[:].rearrange("p (m t) -> p m t", t=PACK),
-                q_raw[:].rearrange("p t (m h) -> p h m t", h=HALVES)[:, h],
-            )
-            q_codes = keep.tile([P, P], U32, name="q_codes%d" % h, tag="q_codes%d" % h, align_bytes=64)
-            q_bytes = keep.tile([P, P], U8, name="q_bytes%d" % h, align_bytes=64)
-            nc.vector.quantize_mx(out=q_codes[:].bitcast(FP8X4), scales=q_bytes[:], in_=q_bf[:])
             bank = psum.tile([P, I], F32, name="scores%d" % h, tag="row%d" % h)
             nc.tensor.matmul_mx(
                 out=bank[:],
-                lhsT=q_codes[:].bitcast(FP8X4),
-                lhsT_scale=q_bytes[:],
+                lhsT=q_codes[:, h * P : (h + 1) * P].bitcast(FP8X4),
+                lhsT_scale=q_bytes[:, h * P : (h + 1) * P],
                 rhs=kg_words[:].bitcast(FP4X4),
                 rhs_scale=kg_bytes[:],
                 start=True,
                 stop=True,
             )
             scores.append(bank)
+
         size_row = psum.tile([P, PACK, P], F32, name="size_row", tag="spread")
         for t in range(PACK):
             nc.tensor.transpose(size_row[:, t, :], size_col[:, t : t + 1].to_broadcast([P, P]), ident[:])
 
-        picks = []
-        pick_tags = ["q_bf1", "q_codes1", "probs1", "q_codes0"]
-
-        def gather_values(j):
-            if j == 3:
-                picked = staged.tile([P, I], BF16, name="v_picked%d" % j, offset=16384)
-            else:
-                picked = keep.tile([P, I], BF16, name="v_picked%d" % j, tag=pick_tags[j], align_bytes=64)
-            nc.vector.tensor_copy(picked[:], v_pool[j][:].indirect(offsets[:]))
-            picks.append(picked)
-            return picked
-
         def turn(rows_bf, name, tag, grouped):
             words = rows_bf[:].bitcast(F32)
-            bank = psum.tile([P, 2, P], F32, name=name + "_bank", tag=tag)
+            bank = psum.tile([P, 2, P], F32, name=name, tag=tag)
             for u in range(2):
                 nc.tensor.transpose(bank[:, u, :], words[:, u::2], ident[:])
             nc.scalar.copy(
@@ -116,27 +106,37 @@ def tile_attend_readerrors_kernel(tc, query, keys_words, keys_scales, size, vals
                 bank[:].rearrange("p u r -> p r u"),
             )
 
-        v_early = keep.tile([P, 2 * P * PACK], BF16, name="v_early", align_bytes=64)
-        v_late = [staged.tile([P, P * PACK], BF16, name="v_late%d" % j, offset=32768 + 1024 * j, align_bytes=64) for j in range(2)]
-        w_turned = keep.tile([P, Q * PACK], BF16, name="w_turned", align_bytes=64)
-        turn(gather_values(0), "v_turned0", "turn_v", v_early[:, 0:I])
+        def gather_and_turn(n, picked, grouped):
+            nc.vector.tensor_copy(picked[:], v_pool[n][:].indirect(offsets[:]))
+            turn(picked, "v_bank%d" % n, "turn_v", grouped)
+
+        v_early = keep.tile([P, 2 * I], BF16, name="v_early", align_bytes=64)
+        picked0 = keep.tile([P, I], BF16, name="picked0", tag="q_bf", align_bytes=64)
+        gather_and_turn(0, picked0, v_early[:, 0:I])
+
+        neg_max, probs, sums = [], [], []
         for h in range(HALVES):
             nm = keep.tile([P, 1], F32, name="neg_max%d" % h)
             nc.vector.tensor_reduce(nm[:], scores[h][:], AXIS.X, ALU.max, negate=True)
             neg_max.append(nm)
-
-        probs, sums = [], []
         for h in range(HALVES):
-            p_h = keep.tile([P, I], F32, name="probs%d" % h, tag="probs%d" % h, align_bytes=64)
+            p_h = keep.tile([P, I], F32, name="probs%d" % h, tag="probs%d" % h)
             s_h = keep.tile([P, 1], F32, name="sums%d" % h)
             nc.scalar.activation(p_h[:], scores[h][:], ACT.Exp, bias=neg_max[h][:], accum_out=s_h[:])
             probs.append(p_h)
             sums.append(s_h)
-        warm = keep.tile([P, 1], F32, name="warm")
-        nc.scalar.activation(warm[:], sums[HALVES - 1][:], ACT.Sqrt)
 
+        tgt_turned = []
+        for b in range(PAIRS):
+            bank = psum.tile([P, 2, HALVES, P], F32, name="tgt_bank%d" % b, tag="turn_w%d" % b)
+            for j in range(2):
+                for h in range(HALVES):
+                    nc.tensor.transpose(bank[:, j, h, :], tgt[:, h, 2 * P * b + j : 2 * P * (b + 1) : 2], ident[:])
+            turned = keep.tile([P, 2, Q], F32, name="tgt_turned%d" % b)
+            nc.scalar.copy(turned[:], bank[:].rearrange("p j h m -> p j (h m)"))
+            tgt_turned.append(turned)
 
-        turn(gather_values(1), "v_turned1", "turn_v", v_early[:, I : 2 * I])
+        w_turned = keep.tile([P, Q * PACK], BF16, name="w_turned", tag="w_turned", align_bytes=64)
         for h in range(HALVES):
             inv = keep.tile([P, 1], F32, name="inv%d" % h)
             nc.vector.reciprocal(inv[:], sums[h][:])
@@ -149,26 +149,27 @@ def tile_attend_readerrors_kernel(tc, query, keys_words, keys_scales, size, vals
                 ALU.mult,
                 ALU.mult,
             )
-            turn(w_bf, "w_turned%d" % h, "turn_w%d" % h, w_turned[:, h * I : (h + 1) * I])
-        turn(gather_values(2), "v_turned2", "turn_v", v_late[0][:])
+            turn(w_bf, "w_bank%d" % h, "turn_w%d" % h, w_turned[:, h * I : (h + 1) * I])
+
+        picked1 = keep.tile([P, I], BF16, name="picked1", tag="probs1")
+        gather_and_turn(1, picked1, v_early[:, I : 2 * I])
+        warm = keep.tile([P, 1], F32, name="warm", tag="probs1")
+        nc.scalar.activation(warm[:], sums[0][:], ACT.Sqrt)
+
         w_codes = keep.tile([P, Q], U32, name="w_codes", align_bytes=64)
         w_bytes = keep.tile([P, Q], U8, name="w_bytes", align_bytes=64)
+        nc.vector.quantize_mx(out=w_codes[:].bitcast(FP8X4), scales=w_bytes[:], in_=w_turned[:])
+
+        v_late = [
+            staged.tile([P, I], BF16, name="v_late%d" % j, offset=BLOCKS * POOL_BYTES + 2 * I * j, align_bytes=64)
+            for j in range(2)
+        ]
+        picked2 = keep.tile([P, I], BF16, name="picked2", tag="w_turned", align_bytes=64)
+        gather_and_turn(2, picked2, v_late[0][:])
+
         early_codes = keep.tile([P, 2 * P], U32, name="early_codes", align_bytes=64)
         early_bytes = keep.tile([P, 2 * P], U8, name="early_bytes", align_bytes=64)
         nc.vector.quantize_mx(out=early_codes[:].bitcast(FP8X4), scales=early_bytes[:], in_=v_early[:])
-        nc.vector.quantize_mx(out=w_codes[:].bitcast(FP8X4), scales=w_bytes[:], in_=w_turned[:])
-
-        tgt_turned = []
-        for pair in range(BLOCKS // 2):
-            bank = psum.tile([P, 2, HALVES, P], F32, name="tgt_bank%d" % pair, tag="row%d" % pair)
-            for jj in range(2):
-                for h in range(HALVES):
-                    nc.tensor.transpose(bank[:, jj, h, :], tgt[:, h, 2 * pair + jj :: BLOCKS], ident[:])
-            turned = keep.tile([P, 2, Q], F32, name="tgt_turned%d" % pair, tag="tgt_turned%d" % pair, align_bytes=64)
-            nc.scalar.copy(turned[:], bank[:].rearrange("p j h m -> p j (h m)"))
-            tgt_turned.append(turned)
-
-        totals = [psum.tile([P, P], F32, name="totals%d" % h, tag="row%d" % h) for h in range(HALVES)]
 
         def read_out(reads, codes, scale_bytes):
             nc.tensor.matmul_mx(
@@ -181,33 +182,47 @@ def tile_attend_readerrors_kernel(tc, query, keys_words, keys_scales, size, vals
                 stop=True,
             )
 
-        def add_turned(j, h, squares):
-            nc.tensor.matmul(totals[h][:], squares, ident[:], start=(j == 0), stop=(j == BLOCKS - 1), is_transpose=True)
+        total_tags = [["row0", "row1"], ["spread", "total"]]
+        totals = [
+            [psum.tile([P, P], F32, name="totals%d_%d" % (b, h), tag=total_tags[b][h]) for h in range(HALVES)]
+            for b in range(PAIRS)
+        ]
 
-        def weigh_and_add(j, plain):
-            sq = keep.tile([P, Q], F32, name="sq%d" % j)
-            nc.scalar.activation(sq[:], plain, ACT.Copy, scale=fw_col[:, j : j + 1])
+        def add_turned(b, j, h, squares):
+            nc.tensor.matmul(totals[b][h][:], squares, ident[:], start=(j == 0), stop=(j == 1), is_transpose=True)
+
+        def weigh_and_add(b, j, plain):
+            sq = keep.tile([P, Q], F32, name="sq%d_%d" % (b, j))
+            nc.scalar.activation(sq[:], plain, ACT.Copy, scale=fw_col[:, b, j : j + 1])
             for h in range(HALVES):
-                add_turned(j, h, sq[:, h * P : (h + 1) * P])
+                add_turned(b, j, h, sq[:, h * P : (h + 1) * P])
 
-        reads_early = psum.tile([P, 2, Q], F32, name="reads_early", tag="read0")
+        def sum_blocks(b):
+            for h in range(HALVES):
+                nc.vector.tensor_reduce(
+                    block_sums[:, h, b, :], totals[b][h][:].rearrange("m (g r) -> m g r", g=G // PAIRS), AXIS.X, ALU.add
+                )
+
+        reads_early = psum.tile([P, 2, Q], F32, name="reads_early", tag="read")
         for j in range(2):
             read_out(reads_early[:, j, :], early_codes[:, j * P : (j + 1) * P], early_bytes[:, j * P : (j + 1) * P])
+        diff_early = keep.tile([P, 2, Q], F32, name="diff_early")
+        nc.vector.tensor_tensor(diff_early[:], reads_early[:], tgt_turned[0][:], ALU.subtract)
+        plain_early = keep.tile([P, 2, Q], F32, name="plain_early")
+        nc.scalar.activation(plain_early[:], diff_early[:], ACT.Square)
+        for j in range(2):
+            weigh_and_add(0, j, plain_early[:, j, :])
 
-        turn(gather_values(3), "v_turned3", "turn_v", v_late[1][:])
+        picked3 = staged.tile([P, I], BF16, name="picked3", offset=2 * POOL_BYTES)
+        gather_and_turn(3, picked3, v_late[1][:])
 
-        codes2 = staged.tile([P, P], U32, name="codes2", offset=24576, align_bytes=64)
+        block_sums = staged.tile([P, HALVES, PAIRS, G // PAIRS], F32, name="block_sums", offset=3 * POOL_BYTES + 4 * P)
+        codes2 = staged.tile([P, P], U32, name="codes2", offset=3 * POOL_BYTES, align_bytes=64)
         bytes2 = keep.tile([P, P], U8, name="bytes2", align_bytes=64)
         nc.vector.quantize_mx(out=codes2[:].bitcast(FP8X4), scales=bytes2[:], in_=v_late[0][:])
         reads2 = psum.tile([P, Q], F32, name="reads2", tag="turn_w0")
         read_out(reads2[:], codes2[:], bytes2[:])
-
-        diff_early = staged.tile([P, 2, Q], F32, name="diff_early", offset=24576 + 1024)
-        nc.vector.tensor_tensor(diff_early[:], reads_early[:], tgt_turned[0][:], ALU.subtract)
-        plain_early = staged.tile([P, 2, Q], F32, name="plain_early", offset=16384)
-        nc.scalar.activation(plain_early[:], diff_early[:], ACT.Square)
-        for j in range(2):
-            weigh_and_add(j, plain_early[:, j, :])
+        sum_blocks(0)
 
         codes3 = keep.tile([P, P], U32, name="codes3", align_bytes=64)
         bytes3 = keep.tile([P, P], U8, name="bytes3", align_bytes=64)
@@ -215,11 +230,11 @@ def tile_attend_readerrors_kernel(tc, query, keys_words, keys_scales, size, vals
         reads3 = psum.tile([P, Q], F32, name="reads3", tag="turn_w1")
         read_out(reads3[:], codes3[:], bytes3[:])
 
-        diff2 = staged.tile([P, Q], F32, name="diff2", offset=32768 + 1024)
+        diff2 = staged.tile([P, Q], F32, name="diff2", offset=BLOCKS * POOL_BYTES + 2 * I)
         nc.vector.tensor_tensor(diff2[:], reads2[:], tgt_turned[1][:, 0, :], ALU.subtract)
         plain2 = keep.tile([P, Q], F32, name="plain2")
         nc.scalar.activation(plain2[:], diff2[:], ACT.Square)
-        weigh_and_add(2, plain2[:])
+        weigh_and_add(1, 0, plain2[:])
 
         diffs = []
         for h in range(HALVES):
@@ -229,16 +244,14 @@ def tile_attend_readerrors_kernel(tc, query, keys_words, keys_scales, size, vals
             diffs.append(diff)
         for h in range(HALVES):
             sq = keep.tile([P, P], F32, name="sq3_%d" % h)
-            nc.vector.scalar_tensor_tensor(sq[:], diffs[h][:], fw_col[:, 3:4], diffs[h][:], ALU.mult, ALU.mult)
-            add_turned(3, h, sq[:])
+            nc.vector.scalar_tensor_tensor(sq[:], diffs[h][:], fw_col[:, 1, 1:2], diffs[h][:], ALU.mult, ALU.mult)
+            add_turned(1, 1, h, sq[:])
+        sum_blocks(1)
 
-        block_sums = keep.tile([P, HALVES, G], F32, name="block_sums")
-        for h in range(HALVES):
-            nc.vector.tensor_reduce(
-                block_sums[:, h, :], totals[h][:].rearrange("m (g r) -> m g r", g=G), AXIS.X, ALU.add
-            )
         roots = keep.tile([P, HALVES * G], F32, name="roots")
-        nc.scalar.activation(roots[:], block_sums[:].rearrange("m h g -> m (h g)"), ACT.Sqrt, scale=16.0 * 16.0 / (E // G))
+        nc.scalar.activation(
+            roots[:], block_sums[:].rearrange("m h b g -> m (h b g)"), ACT.Sqrt, scale=16.0 * 16.0 / (E // G)
+        )
         result = keep.tile([P, HALVES * G], F32, name="result")
         nc.vector.tensor_tensor(result[:], roots[:], tol_sb[:], ALU.subtract)
         nc.sync.dma_start(out.rearrange("(m h) g -> m (h g)", h=HALVES), result[:])

@@ -55,15 +55,15 @@ def tile_attend_readerrors_kernel(tc, query, keys_words, keys_scales, size, vals
         tgt = keep.tile([P, HALVES, E], F32, name="tgt")
         nc.sync.dma_start(v_pool[0][:], vals_by_block[0, 0])
         nc.sync.dma_start(tgt[:], target.rearrange("(m h) e -> m h e", h=HALVES))
+        fw_col = keep.tile([P, PAIRS, 2], F32, name="fw_col")
+        nc.sync.dma_start(fw_col[:], fw.rearrange("o (b p j) -> (o p) b j", b=PAIRS, j=2))
+        tol_sb = keep.tile([P, HALVES * G], F32, name="tol_sb")
+        nc.sync.dma_start(tol_sb[:], tol.rearrange("(m h) g -> m (h g)", h=HALVES))
         for n in range(1, BLOCKS):
             nc.sync.dma_start(v_pool[n][:], vals_by_block[n // 2, n % 2])
 
         ident = keep.tile([P, P], F32, name="ident")
         make_identity(nc, ident[:])
-        fw_col = keep.tile([P, PAIRS, 2], F32, name="fw_col")
-        nc.gpsimd.dma_start(fw_col[:], fw.rearrange("o (b p j) -> (o p) b j", b=PAIRS, j=2))
-        tol_sb = keep.tile([P, HALVES * G], F32, name="tol_sb")
-        nc.gpsimd.dma_start(tol_sb[:], tol.rearrange("(m h) g -> m (h g)", h=HALVES))
 
         kg_words = keep.tile([P, I], U16, name="kg_words", align_bytes=64)
         nc.vector.tensor_copy(kg_words[:], key_words[:].indirect(offsets[:]))
@@ -110,9 +110,12 @@ def tile_attend_readerrors_kernel(tc, query, keys_words, keys_scales, size, vals
             nc.vector.tensor_copy(picked[:], v_pool[n][:].indirect(offsets[:]))
             turn(picked, "v_bank%d" % n, "turn_v", grouped)
 
-        v_early = keep.tile([P, 2 * I], BF16, name="v_early", align_bytes=64)
+        v_turned = [
+            staged.tile([P, I], BF16, name="v_turned%d" % n, offset=BLOCKS * POOL_BYTES + 2 * I * n, align_bytes=64)
+            for n in range(BLOCKS)
+        ]
         picked0 = keep.tile([P, I], BF16, name="picked0", tag="q_bf", align_bytes=64)
-        gather_and_turn(0, picked0, v_early[:, 0:I])
+        gather_and_turn(0, picked0, v_turned[0][:])
 
         neg_max, probs, sums = [], [], []
         for h in range(HALVES):
@@ -136,11 +139,11 @@ def tile_attend_readerrors_kernel(tc, query, keys_words, keys_scales, size, vals
             nc.scalar.copy(turned[:], bank[:].rearrange("p j h m -> p j (h m)"))
             tgt_turned.append(turned)
 
-        w_turned = keep.tile([P, Q * PACK], BF16, name="w_turned", tag="w_turned", align_bytes=64)
+        w_turned = keep.tile([P, Q * PACK], BF16, name="w_turned", align_bytes=64)
         for h in range(HALVES):
             inv = keep.tile([P, 1], F32, name="inv%d" % h)
             nc.vector.reciprocal(inv[:], sums[h][:])
-            w_bf = keep.tile([P, I], BF16, name="w_bf%d" % h)
+            w_bf = staged.tile([P, I], BF16, name="w_bf%d" % h, offset=h * POOL_BYTES)
             nc.vector.scalar_tensor_tensor(
                 w_bf[:].rearrange("q (p t) -> q p t", t=PACK),
                 probs[h][:].rearrange("q (p t) -> q p t", t=PACK),
@@ -150,37 +153,35 @@ def tile_attend_readerrors_kernel(tc, query, keys_words, keys_scales, size, vals
                 ALU.mult,
             )
             turn(w_bf, "w_bank%d" % h, "turn_w%d" % h, w_turned[:, h * I : (h + 1) * I])
+            picked = keep.tile([P, I], BF16, name="picked%d" % (h + 1), tag="probs%d" % h)
+            gather_and_turn(h + 1, picked, v_turned[h + 1][:])
 
-        picked1 = keep.tile([P, I], BF16, name="picked1", tag="probs1")
-        gather_and_turn(1, picked1, v_early[:, I : 2 * I])
-        warm = keep.tile([P, 1], F32, name="warm", tag="probs1")
-        nc.scalar.activation(warm[:], sums[0][:], ACT.Sqrt)
 
-        w_codes = keep.tile([P, Q], U32, name="w_codes", align_bytes=64)
-        w_bytes = keep.tile([P, Q], U8, name="w_bytes", align_bytes=64)
-        nc.vector.quantize_mx(out=w_codes[:].bitcast(FP8X4), scales=w_bytes[:], in_=w_turned[:])
+        def quantise_values(n, codes):
+            scale_bytes = keep.tile([P, P], U8, name="v_bytes%d" % n, align_bytes=64)
+            nc.vector.quantize_mx(out=codes[:].bitcast(FP8X4), scales=scale_bytes[:], in_=v_turned[n][:])
+            return scale_bytes
 
-        v_late = [
-            staged.tile([P, I], BF16, name="v_late%d" % j, offset=BLOCKS * POOL_BYTES + 2 * I * j, align_bytes=64)
-            for j in range(2)
-        ]
-        picked2 = keep.tile([P, I], BF16, name="picked2", tag="w_turned", align_bytes=64)
-        gather_and_turn(2, picked2, v_late[0][:])
-
-        early_codes = keep.tile([P, 2 * P], U32, name="early_codes", align_bytes=64)
-        early_bytes = keep.tile([P, 2 * P], U8, name="early_bytes", align_bytes=64)
-        nc.vector.quantize_mx(out=early_codes[:].bitcast(FP8X4), scales=early_bytes[:], in_=v_early[:])
-
-        def read_out(reads, codes, scale_bytes):
+        def read_out(n, codes, scale_bytes, tag):
+            reads = psum.tile([P, Q], F32, name="reads%d" % n, tag=tag)
             nc.tensor.matmul_mx(
-                out=reads,
-                lhsT=codes.bitcast(FP8X4),
-                lhsT_scale=scale_bytes,
+                out=reads[:],
+                lhsT=codes[:].bitcast(FP8X4),
+                lhsT_scale=scale_bytes[:],
                 rhs=w_codes[:].bitcast(FP8X4),
                 rhs_scale=w_bytes[:],
                 start=True,
                 stop=True,
             )
+            return reads
+
+        w_codes = staged.tile([P, Q], U32, name="w_codes", offset=2 * POOL_BYTES + 4096, align_bytes=64)
+        w_bytes = keep.tile([P, Q], U8, name="w_bytes", align_bytes=64)
+        nc.vector.quantize_mx(out=w_codes[:].bitcast(FP8X4), scales=w_bytes[:], in_=w_turned[:])
+        codes0 = keep.tile([P, P], U32, name="codes0", align_bytes=64)
+        reads0 = read_out(0, codes0, quantise_values(0, codes0), "read")
+        codes1 = keep.tile([P, P], U32, name="codes1", align_bytes=64)
+        reads1 = read_out(1, codes1, quantise_values(1, codes1), "turn_w0")
 
         total_tags = [["row0", "row1"], ["spread", "total"]]
         totals = [
@@ -188,14 +189,19 @@ def tile_attend_readerrors_kernel(tc, query, keys_words, keys_scales, size, vals
             for b in range(PAIRS)
         ]
 
-        def add_turned(b, j, h, squares):
-            nc.tensor.matmul(totals[b][h][:], squares, ident[:], start=(j == 0), stop=(j == 1), is_transpose=True)
+        def add_turned(n, h, squares):
+            nc.tensor.matmul(
+                totals[n // 2][h][:], squares, ident[:], start=(n % 2 == 0), stop=(n % 2 == 1), is_transpose=True
+            )
 
-        def weigh_and_add(b, j, plain):
-            sq = keep.tile([P, Q], F32, name="sq%d_%d" % (b, j))
-            nc.scalar.activation(sq[:], plain, ACT.Copy, scale=fw_col[:, b, j : j + 1])
+        def add_squares(n, reads, diff):
+            nc.vector.tensor_tensor(diff[:], reads[:], tgt_turned[n // 2][:, n % 2, :], ALU.subtract)
+            plain = staged.tile([P, Q], F32, name="plain%d" % n, offset=2 * POOL_BYTES + 512 + 1024 * n)
+            nc.scalar.activation(plain[:], diff[:], ACT.Square)
+            sq = keep.tile([P, Q], F32, name="sq%d" % n)
+            nc.scalar.activation(sq[:], plain[:], ACT.Copy, scale=fw_col[:, n // 2, n % 2 : n % 2 + 1])
             for h in range(HALVES):
-                add_turned(b, j, h, sq[:, h * P : (h + 1) * P])
+                add_turned(n, h, sq[:, h * P : (h + 1) * P])
 
         def sum_blocks(b):
             for h in range(HALVES):
@@ -203,38 +209,24 @@ def tile_attend_readerrors_kernel(tc, query, keys_words, keys_scales, size, vals
                     block_sums[:, h, b, :], totals[b][h][:].rearrange("m (g r) -> m g r", g=G // PAIRS), AXIS.X, ALU.add
                 )
 
-        reads_early = psum.tile([P, 2, Q], F32, name="reads_early", tag="read")
-        for j in range(2):
-            read_out(reads_early[:, j, :], early_codes[:, j * P : (j + 1) * P], early_bytes[:, j * P : (j + 1) * P])
-        diff_early = keep.tile([P, 2, Q], F32, name="diff_early")
-        nc.vector.tensor_tensor(diff_early[:], reads_early[:], tgt_turned[0][:], ALU.subtract)
-        plain_early = keep.tile([P, 2, Q], F32, name="plain_early")
-        nc.scalar.activation(plain_early[:], diff_early[:], ACT.Square)
-        for j in range(2):
-            weigh_and_add(0, j, plain_early[:, j, :])
-
         picked3 = staged.tile([P, I], BF16, name="picked3", offset=2 * POOL_BYTES)
-        gather_and_turn(3, picked3, v_late[1][:])
+        gather_and_turn(3, picked3, v_turned[3][:])
 
-        block_sums = staged.tile([P, HALVES, PAIRS, G // PAIRS], F32, name="block_sums", offset=3 * POOL_BYTES + 4 * P)
         codes2 = staged.tile([P, P], U32, name="codes2", offset=3 * POOL_BYTES, align_bytes=64)
-        bytes2 = keep.tile([P, P], U8, name="bytes2", align_bytes=64)
-        nc.vector.quantize_mx(out=codes2[:].bitcast(FP8X4), scales=bytes2[:], in_=v_late[0][:])
-        reads2 = psum.tile([P, Q], F32, name="reads2", tag="turn_w0")
-        read_out(reads2[:], codes2[:], bytes2[:])
-        sum_blocks(0)
+        reads2 = read_out(2, codes2, quantise_values(2, codes2), "turn_w1")
+        diff0 = staged.tile([P, Q], F32, name="diff0", offset=3 * POOL_BYTES + 1024)
+        add_squares(0, reads0, diff0)
+        diff1 = staged.tile([P, Q], F32, name="diff1", offset=3 * POOL_BYTES + 2048)
+        add_squares(1, reads1, diff1)
 
         codes3 = keep.tile([P, P], U32, name="codes3", align_bytes=64)
-        bytes3 = keep.tile([P, P], U8, name="bytes3", align_bytes=64)
-        nc.vector.quantize_mx(out=codes3[:].bitcast(FP8X4), scales=bytes3[:], in_=v_late[1][:])
-        reads3 = psum.tile([P, Q], F32, name="reads3", tag="turn_w1")
-        read_out(reads3[:], codes3[:], bytes3[:])
-
-        diff2 = staged.tile([P, Q], F32, name="diff2", offset=BLOCKS * POOL_BYTES + 2 * I)
+        reads3 = read_out(3, codes3, quantise_values(3, codes3), "read")
+        diff2 = staged.tile([P, Q], F32, name="diff2", offset=BLOCKS * POOL_BYTES + 2 * I * 3)
         nc.vector.tensor_tensor(diff2[:], reads2[:], tgt_turned[1][:, 0, :], ALU.subtract)
-        plain2 = keep.tile([P, Q], F32, name="plain2")
-        nc.scalar.activation(plain2[:], diff2[:], ACT.Square)
-        weigh_and_add(1, 0, plain2[:])
+        sq2 = keep.tile([P, Q], F32, name="sq2")
+        nc.vector.scalar_tensor_tensor(sq2[:], diff2[:], fw_col[:, 1, 0:1], diff2[:], ALU.mult, ALU.mult)
+        for h in range(HALVES):
+            add_turned(2, h, sq2[:, h * P : (h + 1) * P])
 
         diffs = []
         for h in range(HALVES):
@@ -245,9 +237,11 @@ def tile_attend_readerrors_kernel(tc, query, keys_words, keys_scales, size, vals
         for h in range(HALVES):
             sq = keep.tile([P, P], F32, name="sq3_%d" % h)
             nc.vector.scalar_tensor_tensor(sq[:], diffs[h][:], fw_col[:, 1, 1:2], diffs[h][:], ALU.mult, ALU.mult)
-            add_turned(1, 1, h, sq[:])
-        sum_blocks(1)
+            add_turned(3, h, sq[:])
 
+        block_sums = keep.tile([P, HALVES, PAIRS, G // PAIRS], F32, name="block_sums")
+        for b in range(PAIRS):
+            sum_blocks(b)
         roots = keep.tile([P, HALVES * G], F32, name="roots")
         nc.scalar.activation(
             roots[:], block_sums[:].rearrange("m h b g -> m (h b g)"), ACT.Sqrt, scale=16.0 * 16.0 / (E // G)

from contextlib import ExitStack

import concourse.mybir as mybir
from concourse.masks import make_identity

D, T, I, Q, E, G = 512, 2048, 512, 256, 512, 8
FLOPS = 2 * Q * I * D + 2 * Q * I * E

F32 = mybir.dt.float32
BF16 = mybir.dt.bfloat16
I32 = mybir.dt.int32
U32 = mybir.dt.uint32
U16 = mybir.dt.uint16
U8 = mybir.dt.uint8
FP8X4 = mybir.dt.float8_e4m3fn_x4
FP4X4 = mybir.dt.float4_e2m1fn_x4
ALU = mybir.AluOpType
ACT = mybir.ActivationFunctionType
AXIS = mybir.AxisListType

P = 128
PACK = 4
HALVES = Q // P
PAIRS = 2
BLOCKS = E // P
POOL_BYTES = 4 * T


def tile_attend_readerrors_kernel(tc, query, keys_words, keys_scales, size, vals, target, fw, tol, offs, out):
    nc = tc.nc
    with ExitStack() as ctx:
        keep = ctx.enter_context(tc.tile_pool(name="keep", bufs=1))
        staged = ctx.enter_context(tc.tile_pool(name="staged", bufs=1))
        psum = ctx.enter_context(tc.psum_pool(name="psum", bufs=1))

        offsets = keep.tile([P, I // 16], U16, name="offsets")
        nc.sync.dma_start(offsets[:], offs)

        key_bytes = keep.tile([P, T], U8, name="key_bytes")
        nc.gpsimd.memset(key_bytes[:].bitcast(I32), 0)
        for quad in range(4):
            (nc.scalar if quad < 2 else nc.sync).dma_start(
                key_bytes[32 * quad : 32 * quad + 4, :].bitcast(I32),
                keys_scales[0, 4 * quad : 4 * quad + 4, :].bitcast(I32),
            )
        key_words = keep.tile([P, T], U16, name="key_words")
        nc.sync.dma_start(key_words[:].bitcast(I32), keys_words[0].bitcast(I32))
        q_raw = keep.tile([P, PACK, Q], F32, name="q_raw")
        nc.sync.dma_start(q_raw[:], query.rearrange("(p t) q -> p t q", t=PACK))
        size_col = keep.tile([P, PACK], F32, name="size_col")
        nc.sync.dma_start(size_col[:], size.rearrange("o (p t) -> (o p) t", t=PACK))

        vals_by_block = vals.rearrange("(b p j) t -> b j p t", b=PAIRS, j=2)
        v_pool = [staged.tile([P, T], F32, name="v_pool%d" % n, offset=POOL_BYTES * n) for n in range(BLOCKS)]
        tgt = keep.tile([P, HALVES, E], F32, name="tgt")
        nc.sync.dma_start(v_pool[0][:], vals_by_block[0, 0])
        nc.sync.dma_start(tgt[:], target.rearrange("(m h) e -> m h e", h=HALVES))
        fw_col = keep.tile([P, PAIRS, 2], F32, name="fw_col")
        nc.sync.dma_start(fw_col[:], fw.rearrange("o (b p j) -> (o p) b j", b=PAIRS, j=2))
        tol_sb = keep.tile([P, HALVES * G], F32, name="tol_sb")
        nc.sync.dma_start(tol_sb[:], tol.rearrange("(m h) g -> m (h g)", h=HALVES))
        for n in range(1, BLOCKS):
            nc.sync.dma_start(v_pool[n][:], vals_by_block[n // 2, n % 2])

        ident = keep.tile([P, P], F32, name="ident")
        make_identity(nc, ident[:])

        kg_words = keep.tile([P, I], U16, name="kg_words", align_bytes=64)
        nc.vector.tensor_copy(kg_words[:], key_words[:].indirect(offsets[:]))
        kg_bytes = keep.tile([P, I], U8, name="kg_bytes", align_bytes=64)
        nc.vector.tensor_copy(kg_bytes[:], key_bytes[:].indirect(offsets[:]))

        q_bf = keep.tile([P, Q * PACK], BF16, name="q_bf", tag="q_bf", align_bytes=64)
        nc.scalar.copy(
            q_bf[:].rearrange("p (h m t) -> p m h t", h=HALVES, t=PACK),
            q_raw[:].rearrange("p t (m h) -> p m h t", h=HALVES),
        )
        q_codes = keep.tile([P, Q], U32, name="q_codes", align_bytes=64)
        q_bytes = keep.tile([P, Q], U8, name="q_bytes", align_bytes=64)
        nc.vector.quantize_mx(out=q_codes[:].bitcast(FP8X4), scales=q_bytes[:], in_=q_bf[:])
        scores = []
        for h in range(HALVES):
            bank = psum.tile([P, I], F32, name="scores%d" % h, tag="row%d" % h)
            nc.tensor.matmul_mx(
                out=bank[:],
                lhsT=q_codes[:, h * P : (h + 1) * P].bitcast(FP8X4),
                lhsT_scale=q_bytes[:, h * P : (h + 1) * P],
                rhs=kg_words[:].bitcast(FP4X4),
                rhs_scale=kg_bytes[:],
                start=True,
                stop=True,
            )
            scores.append(bank)

        size_row = psum.tile([P, PACK, P], F32, name="size_row", tag="spread")
        for t in range(PACK):
            nc.tensor.transpose(size_row[:, t, :], size_col[:, t : t + 1].to_broadcast([P, P]), ident[:])

        def turn(rows_bf, name, tag, grouped):
            words = rows_bf[:].bitcast(F32)
            bank = psum.tile([P, 2, P], F32, name=name, tag=tag)
            for u in range(2):
                nc.tensor.transpose(bank[:, u, :], words[:, u::2], ident[:])
            nc.scalar.copy(
                grouped.bitcast(F32).rearrange("p (r u) -> p r u", u=2),
                bank[:].rearrange("p u r -> p r u"),
            )

        def gather_and_turn(n, picked, grouped):
            nc.vector.tensor_copy(picked[:], v_pool[n][:].indirect(offsets[:]))
            turn(picked, "v_bank%d" % n, "turn_v", grouped)

        v_turned = [
            staged.tile([P, I], BF16, name="v_turned%d" % n, offset=BLOCKS * POOL_BYTES + 2 * I * n, align_bytes=64)
            for n in range(BLOCKS)
        ]
        picked0 = keep.tile([P, I], BF16, name="picked0", tag="q_bf", align_bytes=64)
        gather_and_turn(0, picked0, v_turned[0][:])

        neg_max, probs, sums = [], [], []
        for h in range(HALVES):
            nm = keep.tile([P, 1], F32, name="neg_max%d" % h)
            nc.vector.tensor_reduce(nm[:], scores[h][:], AXIS.X, ALU.max, negate=True)
            neg_max.append(nm)
        for h in range(HALVES):
            p_h = keep.tile([P, I], F32, name="probs%d" % h, tag="probs%d" % h)
            s_h = keep.tile([P, 1], F32, name="sums%d" % h)
            nc.scalar.activation(p_h[:], scores[h][:], ACT.Exp, bias=neg_max[h][:], accum_out=s_h[:])
            probs.append(p_h)
            sums.append(s_h)

        tgt_turned = []
        for b in range(PAIRS):
            bank = psum.tile([P, 2, HALVES, P], F32, name="tgt_bank%d" % b, tag="turn_w%d" % b)
            for j in range(2):
                for h in range(HALVES):
                    nc.tensor.transpose(bank[:, j, h, :], tgt[:, h, 2 * P * b + j : 2 * P * (b + 1) : 2], ident[:])
            turned = keep.tile([P, 2, Q], F32, name="tgt_turned%d" % b)
            nc.scalar.copy(turned[:], bank[:].rearrange("p j h m -> p j (h m)"))
            tgt_turned.append(turned)

        w_turned = keep.tile([P, Q * PACK], BF16, name="w_turned", align_bytes=64)
        for h in range(HALVES):
            inv = keep.tile([P, 1], F32, name="inv%d" % h)
            nc.vector.reciprocal(inv[:], sums[h][:])
            w_bf = staged.tile([P, I], BF16, name="w_bf%d" % h, offset=h * POOL_BYTES)
            nc.vector.scalar_tensor_tensor(
                w_bf[:].rearrange("q (p t) -> q p t", t=PACK),
                probs[h][:].rearrange("q (p t) -> q p t", t=PACK),
                inv[:],
                size_row[:].rearrange("q t p -> q p t"),
                ALU.mult,
                ALU.mult,
            )
            turn(w_bf, "w_bank%d" % h, "turn_w%d" % h, w_turned[:, h * I : (h + 1) * I])
            picked = keep.tile([P, I], BF16, name="picked%d" % (h + 1), tag="probs%d" % h)
            gather_and_turn(h + 1, picked, v_turned[h + 1][:])


        def quantise_values(n, codes):
            scale_bytes = keep.tile([P, P], U8, name="v_bytes%d" % n, align_bytes=64)
            nc.vector.quantize_mx(out=codes[:].bitcast(FP8X4), scales=scale_bytes[:], in_=v_turned[n][:])
            return scale_bytes

        def read_out(n, codes, scale_bytes, tag):
            reads = psum.tile([P, Q], F32, name="reads%d" % n, tag=tag)
            nc.tensor.matmul_mx(
                out=reads[:],
                lhsT=codes[:].bitcast(FP8X4),
                lhsT_scale=scale_bytes[:],
                rhs=w_codes[:].bitcast(FP8X4),
                rhs_scale=w_bytes[:],
                start=True,
                stop=True,
            )
            return reads

        w_codes = staged.tile([P, Q], U32, name="w_codes", offset=2 * POOL_BYTES + 4096, align_bytes=64)
        w_bytes = keep.tile([P, Q], U8, name="w_bytes", align_bytes=64)
        nc.vector.quantize_mx(out=w_codes[:].bitcast(FP8X4), scales=w_bytes[:], in_=w_turned[:])
        codes0 = keep.tile([P, P], U32, name="codes0", align_bytes=64)
        reads0 = read_out(0, codes0, quantise_values(0, codes0), "read")
        codes1 = keep.tile([P, P], U32, name="codes1", align_bytes=64)
        reads1 = read_out(1, codes1, quantise_values(1, codes1), "turn_w0")

        total_tags = [["row0", "row1"], ["spread", "total"]]
        totals = [
            [psum.tile([P, P], F32, name="totals%d_%d" % (b, h), tag=total_tags[b][h]) for h in range(HALVES)]
            for b in range(PAIRS)
        ]

        def add_turned(n, h, squares):
            nc.tensor.matmul(
                totals[n // 2][h][:], squares, ident[:], start=(n % 2 == 0), stop=(n % 2 == 1), is_transpose=True
            )

        def add_squares(n, reads, diff):
            nc.vector.tensor_tensor(diff[:], reads[:], tgt_turned[n // 2][:, n % 2, :], ALU.subtract)
            plain = staged.tile([P, Q], F32, name="plain%d" % n, offset=2 * POOL_BYTES + 512 + 1024 * n)
            nc.scalar.activation(plain[:], diff[:], ACT.Square)
            sq = keep.tile([P, Q], F32, name="sq%d" % n)
            nc.scalar.activation(sq[:], plain[:], ACT.Copy, scale=fw_col[:, n // 2, n % 2 : n % 2 + 1])
            for h in range(HALVES):
                add_turned(n, h, sq[:, h * P : (h + 1) * P])

        def sum_blocks(b):
            for h in range(HALVES):
                nc.vector.tensor_reduce(
                    block_sums[:, h, b, :], totals[b][h][:].rearrange("m (g r) -> m g r", g=G // PAIRS), AXIS.X, ALU.add
                )

        picked3 = staged.tile([P, I], BF16, name="picked3", offset=2 * POOL_BYTES)
        gather_and_turn(3, picked3, v_turned[3][:])

        codes2 = staged.tile([P, P], U32, name="codes2", offset=3 * POOL_BYTES, align_bytes=64)
        reads2 = read_out(2, codes2, quantise_values(2, codes2), "turn_w1")
        diff0 = staged.tile([P, Q], F32, name="diff0", offset=3 * POOL_BYTES + 1024)
        add_squares(0, reads0, diff0)
        diff1 = staged.tile([P, Q], F32, name="diff1", offset=3 * POOL_BYTES + 2048)
        add_squares(1, reads1, diff1)

        codes3 = keep.tile([P, P], U32, name="codes3", align_bytes=64)
        reads3 = read_out(3, codes3, quantise_values(3, codes3), "read")
        diff2 = staged.tile([P, Q], F32, name="diff2", offset=BLOCKS * POOL_BYTES + 2 * I * 3)
        nc.vector.tensor_tensor(diff2[:], reads2[:], tgt_turned[1][:, 0, :], ALU.subtract)
        sq2 = keep.tile([P, Q], F32, name="sq2")
        nc.vector.scalar_tensor_tensor(sq2[:], diff2[:], fw_col[:, 1, 0:1], diff2[:], ALU.mult, ALU.mult)
        for h in range(HALVES):
            add_turned(2, h, sq2[:, h * P : (h + 1) * P])

        diffs = []
        for h in range(HALVES):
            diff = keep.tile([P, P], F32, name="diff3_%d" % h)
            cols = slice(h * P, (h + 1) * P)
            nc.vector.tensor_tensor(diff[:], reads3[:, cols], tgt_turned[1][:, 1, cols], ALU.subtract)
            diffs.append(diff)
        for h in range(HALVES):
            sq = keep.tile([P, P], F32, name="sq3_%d" % h)
            nc.vector.scalar_tensor_tensor(sq[:], diffs[h][:], fw_col[:, 1, 1:2], diffs[h][:], ALU.mult, ALU.mult)
            add_turned(3, h, sq[:])

        block_sums = keep.tile([P, HALVES, PAIRS, G // PAIRS], F32, name="block_sums")
        for b in range(PAIRS):
            sum_blocks(b)
        roots = keep.tile([P, HALVES * G], F32, name="roots")
        nc.scalar.activation(
            roots[:], block_sums[:].rearrange("m h b g -> m (h b g)"), ACT.Sqrt, scale=16.0 * 16.0 / (E // G)
        )
        result = keep.tile([P, HALVES * G], F32, name="result")
        nc.vector.tensor_tensor(result[:], roots[:], tol_sb[:], ALU.subtract)
        nc.sync.dma_start(out.rearrange("(m h) g -> m (h g)", h=HALVES), result[:])
